import numpy as np
import ml_dtypes


def mxq(x, axis, fmt="e4m3"):
    dtype, down = {"e4m3": (ml_dtypes.float8_e4m3fn, 7), "e5m2": (ml_dtypes.float8_e5m2, 14)}[fmt]
    v = np.moveaxis(np.asarray(x, np.float32).astype(ml_dtypes.bfloat16).astype(np.float64), axis, -1)
    blocks = v.reshape(v.shape[:-1] + (-1, 32))
    amax = np.abs(blocks).max(-1, keepdims=True)
    byte = np.maximum(np.where(amax > 0, np.frexp(amax)[1] - 1 + 127, 0) - down, 1)
    scale = np.exp2(byte - 127.0)
    codes = (blocks / scale).astype(np.float32).astype(dtype).astype(np.float64)
    return np.moveaxis((codes * scale).reshape(v.shape), -1, axis)


WIDE = False


def mx_kscale(k):
    if not WIDE:
        return np.ones(k)
    levels = np.array([10, -10, 5, -5, 0])
    if k % 512:
        return np.exp2(np.random.permutation(np.resize(levels, k // 32))).repeat(32)
    a = np.empty((k // 512, 16))
    for p in range(k // 512):
        a[p, :8] = np.random.permutation(np.resize(levels, 8))
        for g in range(8):
            far = levels[np.abs(levels - a[p, g]) >= 10]
            a[p, g + 8] = far[np.random.randint(len(far))]
    return np.exp2(a.ravel()).repeat(32)


def f64(x):
    return np.asarray(x).astype(np.float64)


def striped(idx):
    return np.tile(idx.reshape(-1, 16).T, (8, 1)).astype(np.uint16)


def unstriped(offs):
    return offs[:16].T.reshape(-1).astype(np.int64)


def silu(v):
    return v / (1.0 + np.exp(-np.maximum(v, -700.0)))


K, T, S, V, H, N, J, U = 1024, 2048, 512, 256, 512, 256, 512, 512


def setup_inputs():
    n = np.random.standard_normal
    s = mx_kscale(K)[:, None]
    u = mx_kscale(H)
    r = mx_kscale(J)[:, None]
    return {
        "xT": (n((K, T)) * s).astype(np.float32),
        "aT": (n((J, U)) * r).astype(np.float32),
        "w1": (n((K, H)) / np.sqrt(K) / s * u).astype(np.float32),
        "w3": (n((J, H)) / np.sqrt(J) / r).astype(np.float32),
        "w2": (n((H, N)) / np.sqrt(2 * H) / u[:, None]).astype(np.float32),
        "offs": striped(np.random.permutation(T)[:S]),
        "pos1": striped(np.random.permutation(S)[:V]),
        "pos2": striped(np.random.permutation(S)[:V]),
    }


def reference(xT, aT, w1, w3, w2, offs, pos1, pos2):
    xq = mxq(f64(xT)[:, unstriped(offs)], 0, "e4m3")
    h = silu(mxq(f64(w1), 0, "e4m3").T @ xq)
    f = mxq(f64(w3), 0, "e4m3").T @ mxq(f64(aT), 0, "e4m3")
    z = h[:, unstriped(pos1)] * f[:, :V] + h[:, unstriped(pos2)] * f[:, V:2 * V]
    return mxq(f64(w2), 0, "e4m3").T @ mxq(z, 0, "e4m3")

@@ -1,0 +1,141 @@
+from contextlib import ExitStack
+
+import concourse.mybir as mybir
+
+K, T, S, V, H, N, J = 1024, 2048, 512, 256, 512, 256, 512
+FLOPS = 2 * (K * H * S + J * H * 2 * V + H * N * V)
+
+F32 = mybir.dt.float32
+BF16 = mybir.dt.bfloat16
+U32 = mybir.dt.uint32
+U16 = mybir.dt.uint16
+U8 = mybir.dt.uint8
+FP8X4 = mybir.dt.float8_e4m3fn_x4
+SILU = mybir.ActivationFunctionType.Silu
+MULT = mybir.AluOpType.mult
+ADD = mybir.AluOpType.add
+
+P = 128
+PACK = 4
+K_PASS = P * PACK
+
+
+def tile_picked_dime_none_e_kernel(tc, xT, aT, w1, w3, w2, offs, pos1, pos2, out):
+    nc = tc.nc
+    passes = K // K_PASS
+
+    with ExitStack() as ctx:
+        keep = ctx.enter_context(tc.tile_pool(name="keep", bufs=1))
+        psum = ctx.enter_context(tc.psum_pool(name="psum", bufs=1))
+
+        def tile(name, shape, dtype):
+            return keep.tile(shape, dtype, name=name, align_bytes=64)
+
+        def quantize(name, grouped):
+            width = grouped.shape[1]
+            codes = tile(name + "_codes", [P, width], U32)
+            scales = tile(name + "_scales", [P, width], U8)
+            nc.vector.quantize_mx(
+                out=codes[:].bitcast(FP8X4), scales=scales[:], in_=grouped[:].rearrange("p w j -> p (w j)")
+            )
+            return codes, scales
+
+        def matmul(acc, lhs, rhs, start, stop):
+            nc.tensor.matmul_mx(
+                out=acc, lhsT=lhs[0].bitcast(FP8X4), lhsT_scale=lhs[1],
+                rhs=rhs[0].bitcast(FP8X4), rhs_scale=rhs[1], start=start, stop=stop,
+            )
+
+        def copy(on_vector, dst, src):
+            if on_vector:
+                nc.vector.tensor_copy(out=dst, in_=src)
+            else:
+                nc.scalar.copy(out=dst, in_=src)
+
+        def group_columns(name, raw, on_vector):
+            width = raw.shape[2]
+            grouped = tile(name, [P, width, PACK], BF16)
+            copy(on_vector,
+                 grouped[:].rearrange("p (c i) j -> p c j i", i=4),
+                 raw.rearrange("p j (c i) -> p c j i", i=4))
+            return grouped
+
+        def group_channels(name, raw, t, on_vector):
+            grouped = tile(name, [P, P, PACK], BF16)
+            copy(on_vector,
+                 grouped[:].rearrange("p (g h i) j -> p g h j i", h=2, i=4),
+                 raw[:].rearrange("p j (g t h i) -> p t g h j i", t=PACK, h=2, i=4)[:, t])
+            return grouped
+
+        def load_rows(name, rows):
+            raw = tile(name, [P, PACK, rows.shape[1]], F32)
+            nc.sync.dma_start(out=raw[:], in_=rows.rearrange("(p j) w -> p j w", j=PACK))
+            return raw
+
+        def load_list(name, src):
+            lst = keep.tile(list(src.shape), U16, name=name)
+            nc.sync.dma_start(lst[:], src)
+            return lst
+
+        x_rows = xT.rearrange("(z p j) w -> z j p w", p=P, j=PACK)
+        planes = {}
+        for z in range(passes):
+            for j in range(PACK):
+                planes[z, j] = tile("x%d%d" % (z, j), [P, T], F32)
+                nc.sync.dma_start(out=planes[z, j][:], in_=x_rows[z, j])
+                if (z, j) == (0, 0):
+                    picks = load_list("picks", offs)
+                if (z, j) == (0, 1):
+                    places = [load_list("places1", pos1), load_list("places2", pos2)]
+        w1_raw = [load_rows("w1_raw%d" % z, w1[z * K_PASS:(z + 1) * K_PASS, :]) for z in range(passes)]
+        a_raw = load_rows("a_raw", aT)
+        w3_raw = load_rows("w3_raw", w3)
+        w2_raw = tile("w2_raw", [P, PACK, N], F32)
+        w2_rows = w2.rearrange("(g t e) n -> t g e n", t=PACK, e=8)
+        for t in range(PACK):
+            nc.sync.dma_start(out=w2_raw[:, t, :], in_=w2_rows[t])
+
+        x_q = []
+        for z in range(passes):
+            grouped = tile("x_grouped%d" % z, [P, S, PACK], BF16)
+            for j in range(PACK):
+                nc.vector.tensor_copy(out=grouped[:, :, j], in_=planes[z, j][:].indirect(picks[:]))
+            x_q.append(quantize("x%d" % z, grouped))
+
+        h_acc = [psum.tile([P, S], F32, name="h_acc%d" % t, tag="bank%d" % t) for t in range(PACK)]
+        h = [tile("h%d" % t, [P, S], F32) for t in range(PACK)]
+        for z in range(passes):
+            grouped = [group_channels("w1_g%d%d" % (z, t), w1_raw[z], t, t in (1, 2)) for t in range(PACK)]
+            for t in range(PACK):
+                codes, scales = quantize("w1_%d%d" % (z, t), grouped[t])
+                matmul(h_acc[t][:], (codes[:], scales[:]), (x_q[z][0][:], x_q[z][1][:]), z == 0, z == passes - 1)
+        fetched = [tile("fetched%d" % t, [P, 2 * V], F32) for t in range(PACK)]
+        for t in range(PACK):
+            nc.scalar.activation(out=h[t][:], in_=h_acc[t][:], func=SILU)
+            for d in range(2):
+                nc.vector.tensor_copy(out=fetched[t][:, d * V:(d + 1) * V], in_=h[t][:].indirect(places[d][:]))
+
+        a_q = quantize("a", group_columns("a_g", a_raw[:], False))
+        terms = tile("terms", [P, PACK, 2 * V], F32)
+        for t in range(PACK):
+            codes, scales = quantize("w3_%d" % t, group_channels("w3_g%d" % t, w3_raw, t, False))
+            f_acc = psum.tile([P, 2 * V], F32, name="f_acc%d" % t, tag="bank%d" % (PACK + t))
+            matmul(f_acc[:], (codes[:], scales[:]), (a_q[0][:], a_q[1][:]), True, True)
+            nc.vector.tensor_tensor(out=terms[:, t, :], in0=fetched[t][:], in1=f_acc[:], op=MULT)
+        w2_codes, w2_scales = quantize("w2", group_columns("w2_g", w2_raw[:], False))
+
+        z_grouped = tile("z_grouped", [P, V, PACK], BF16)
+        nc.vector.tensor_tensor(
+            out=z_grouped[:].rearrange("p (c i) t -> p c t i", i=4),
+            in0=terms[:, :, 0:V].rearrange("p t (c i) -> p c t i", i=4),
+            in1=terms[:, :, V:2 * V].rearrange("p t (c i) -> p c t i", i=4),
+            op=ADD,
+        )
+        z_q = quantize("z", z_grouped)
+        for a in range(N // P):
+            rows = slice(a * P, (a + 1) * P)
+            acc = psum.tile([P, V], F32, name="out_acc%d" % a, tag="bank%d" % a)
+            matmul(acc[:], (w2_codes[:, rows], w2_scales[:, rows]), (z_q[0][:], z_q[1][:]), True, True)
+            result = tile("result%d" % a, [P, V], F32)
+            copy(a == 1, result[:], acc[:])
+            (nc.sync if a == 1 else nc.scalar).dma_start(out=out[rows, :], in_=result[:])

@@ -28,15 +28,15 @@ def tile_picked_dime_none_e_kernel(tc, xT, aT, w1, w3, w2, offs, pos1, pos2, out
         keep = ctx.enter_context(tc.tile_pool(name="keep", bufs=1))
         psum = ctx.enter_context(tc.psum_pool(name="psum", bufs=1))
 
-        def tile(name, shape, dtype):
-            return keep.tile(shape, dtype, name=name, align_bytes=64)
+        def tile(name, shape, dtype, tag=None):
+            return keep.tile(shape, dtype, name=name, tag=tag or name, align_bytes=64)
 
-        def quantize(name, grouped):
+        def quantize(name, grouped, tag=None):
             width = grouped.shape[1]
-            codes = tile(name + "_codes", [P, width], U32)
+            codes = tile(name + "_codes", [P, width], U32, tag=tag)
             scales = tile(name + "_scales", [P, width], U8)
             nc.vector.quantize_mx(
-                out=codes[:].bitcast(FP8X4), scales=scales[:], in_=grouped[:].rearrange("p w j -> p (w j)")
+                out=codes[:].bitcast(FP8X4), scales=scales[:], in_=grouped.rearrange("p w j -> p (w j)")
             )
             return codes, scales
 
@@ -58,12 +58,11 @@ def tile_picked_dime_none_e_kernel(tc, xT, aT, w1, w3, w2, offs, pos1, pos2, out
             copy(on_vector,
                  grouped[:].rearrange("p (c i) j -> p c j i", i=4),
                  raw.rearrange("p j (c i) -> p c j i", i=4))
-            return grouped
+            return grouped[:]
 
-        def group_channels(name, raw, t, on_vector):
-            grouped = tile(name, [P, P, PACK], BF16)
+        def group_channels(grouped, raw, t, on_vector):
             copy(on_vector,
-                 grouped[:].rearrange("p (g h i) j -> p g h j i", h=2, i=4),
+                 grouped.rearrange("p (g h i) j -> p g h j i", h=2, i=4),
                  raw[:].rearrange("p j (g t h i) -> p t g h j i", t=PACK, h=2, i=4)[:, t])
             return grouped
 
@@ -77,6 +76,10 @@ def tile_picked_dime_none_e_kernel(tc, xT, aT, w1, w3, w2, offs, pos1, pos2, out
             nc.sync.dma_start(lst[:], src)
             return lst
 
+        warm = tile("warm", [P, 8], F32)
+        nc.vector.memset(warm[:], 0.0)
+        warm2 = tile("warm2", [P, 8], F32)
+        nc.scalar.activation(out=warm2[:], in_=warm[:], func=SILU)
         x_rows = xT.rearrange("(z p j) w -> z j p w", p=P, j=PACK)
         planes = {}
         for z in range(passes):
@@ -88,54 +91,99 @@ def tile_picked_dime_none_e_kernel(tc, xT, aT, w1, w3, w2, offs, pos1, pos2, out
                 if (z, j) == (0, 1):
                     places = [load_list("places1", pos1), load_list("places2", pos2)]
         w1_raw = [load_rows("w1_raw%d" % z, w1[z * K_PASS:(z + 1) * K_PASS, :]) for z in range(passes)]
-        a_raw = load_rows("a_raw", aT)
+        a_raw = [load_rows("a_raw0", aT[:, 0:V])]
         w3_raw = load_rows("w3_raw", w3)
+        a_raw.append(load_rows("a_raw1", aT[:, V:2 * V]))
         w2_raw = tile("w2_raw", [P, PACK, N], F32)
         w2_rows = w2.rearrange("(g t e) n -> t g e n", t=PACK, e=8)
         for t in range(PACK):
             nc.sync.dma_start(out=w2_raw[:, t, :], in_=w2_rows[t])
 
+        x_grouped = [tile("x_grouped%d" % z, [P, S, PACK], BF16) for z in range(passes)]
         x_q = []
         for z in range(passes):
-            grouped = tile("x_grouped%d" % z, [P, S, PACK], BF16)
             for j in range(PACK):
-                nc.vector.tensor_copy(out=grouped[:, :, j], in_=planes[z, j][:].indirect(picks[:]))
-            x_q.append(quantize("x%d" % z, grouped))
+                nc.vector.tensor_copy(out=x_grouped[z][:, :, j], in_=planes[z, j][:].indirect(picks[:]))
 
-        h_acc = [psum.tile([P, S], F32, name="h_acc%d" % t, tag="bank%d" % t) for t in range(PACK)]
+        def bank(name, b, width):
+            return psum.tile([P, width], F32, name=name, tag="bank%d" % b)
+
+        h_parts = [[(slice(0, S // 2), 0), (slice(S // 2, S), PACK)]] + [[(slice(0, S), t)] for t in range(1, PACK)]
+        h_acc = [[bank("h_acc%d" % b, b, cols.stop - cols.start) for cols, b in parts] for parts in h_parts]
         h = [tile("h%d" % t, [P, S], F32) for t in range(PACK)]
         for z in range(passes):
-            grouped = [group_channels("w1_g%d%d" % (z, t), w1_raw[z], t, t in (1, 2)) for t in range(PACK)]
+            x_q.append(quantize("x%d" % z, x_grouped[z][:], tag="w1_g02" if z == 1 else None))
             for t in range(PACK):
-                codes, scales = quantize("w1_%d%d" % (z, t), grouped[t])
-                matmul(h_acc[t][:], (codes[:], scales[:]), (x_q[z][0][:], x_q[z][1][:]), z == 0, z == passes - 1)
-        fetched = [tile("fetched%d" % t, [P, 2 * V], F32) for t in range(PACK)]
-        for t in range(PACK):
-            nc.scalar.activation(out=h[t][:], in_=h_acc[t][:], func=SILU)
+                grouped = group_channels(tile("w1_g%d%d" % (z, t), [P, P, PACK], BF16)[:], w1_raw[z], t, t % 2 == 0)
+                codes, scales = quantize("w1_%d%d" % (z, t), grouped)
+                for (cols, b), acc in zip(h_parts[t], h_acc[t]):
+                    matmul(acc[:], (codes[:], scales[:]), (x_q[z][0][:, cols], x_q[z][1][:, cols]), z == 0, z == passes - 1)
+
+        fetched = []
+        terms_flat = tile("terms", [P, PACK * 2 * V], F32)
+        terms = terms_flat[:].rearrange("p (t v) -> p t v", t=PACK)
+        a_grouped = [tile("a_grouped%d" % d, [P, V, PACK], BF16) for d in range(2)]
+        a_codes = tile("a_codes", [P, 2 * V], U32)
+        a_scales = tile("a_scales", [P, 2 * V], U8)
+
+        def fetch(t):
+            for (cols, b), acc in zip(h_parts[t], h_acc[t]):
+                nc.scalar.activation(out=h[t][:, cols], in_=acc[:], func=SILU)
+            fetched.append(tile("fetched%d" % t, [P, 2 * V], F32, tag="a_grouped1" if t == PACK - 1 else None))
             for d in range(2):
                 nc.vector.tensor_copy(out=fetched[t][:, d * V:(d + 1) * V], in_=h[t][:].indirect(places[d][:]))
 
-        a_q = quantize("a", group_columns("a_g", a_raw[:], False))
-        terms = tile("terms", [P, PACK, 2 * V], F32)
+        def angles(d):
+            cols = slice(d * V, (d + 1) * V)
+            copy(d == 0, a_grouped[d][:].rearrange("p (c i) j -> p c j i", i=4),
+                 a_raw[d][:].rearrange("p j (c i) -> p c j i", i=4))
+            nc.vector.quantize_mx(out=a_codes[:, cols].bitcast(FP8X4), scales=a_scales[:, cols],
+                                  in_=a_grouped[d][:].rearrange("p w j -> p (w j)"))
+
+        def filters(pair, staged):
+            for e in range(2):
+                group_channels(staged[:, e * P:(e + 1) * P, :], w3_raw, 2 * pair + e, False)
+            return quantize("w3_%d" % pair, staged)
+
+        def filter_products(pair, w3_q):
+            accs = []
+            for e in range(2):
+                acc = bank("f_acc%d%d" % (pair, e), PACK + 2 * pair + e, 2 * V)
+                cols = slice(e * P, (e + 1) * P)
+                matmul(acc[:], (w3_q[0][:, cols], w3_q[1][:, cols]), (a_codes[:], a_scales[:]), True, True)
+                accs.append(acc)
+            return accs
+
+        angles(0)
+        fetch(0)
+        fetch(1)
+        w3_first = filters(0, tile("w3_g0", [P, 2 * P, PACK], BF16)[:])
+        fetch(2)
+        angles(1)
+        f_acc = filter_products(0, w3_first)
+        fetch(3)
+        staged = terms_flat[:, 0:2 * V].bitcast(BF16).rearrange("p (m j) -> p m j", j=PACK)
+        f_acc.extend(filter_products(1, filters(1, staged)))
         for t in range(PACK):
-            codes, scales = quantize("w3_%d" % t, group_channels("w3_g%d" % t, w3_raw, t, False))
-            f_acc = psum.tile([P, 2 * V], F32, name="f_acc%d" % t, tag="bank%d" % (PACK + t))
-            matmul(f_acc[:], (codes[:], scales[:]), (a_q[0][:], a_q[1][:]), True, True)
-            nc.vector.tensor_tensor(out=terms[:, t, :], in0=fetched[t][:], in1=f_acc[:], op=MULT)
+            nc.vector.tensor_tensor(out=terms_flat[:, t * 2 * V:(t + 1) * 2 * V], in0=fetched[t][:], in1=f_acc[t][:], op=MULT)
         w2_codes, w2_scales = quantize("w2", group_columns("w2_g", w2_raw[:], False))
 
-        z_grouped = tile("z_grouped", [P, V, PACK], BF16)
-        nc.vector.tensor_tensor(
-            out=z_grouped[:].rearrange("p (c i) t -> p c t i", i=4),
-            in0=terms[:, :, 0:V].rearrange("p t (c i) -> p c t i", i=4),
-            in1=terms[:, :, V:2 * V].rearrange("p t (c i) -> p c t i", i=4),
-            op=ADD,
-        )
-        z_q = quantize("z", z_grouped)
-        for a in range(N // P):
-            rows = slice(a * P, (a + 1) * P)
-            acc = psum.tile([P, V], F32, name="out_acc%d" % a, tag="bank%d" % a)
-            matmul(acc[:], (w2_codes[:, rows], w2_scales[:, rows]), (z_q[0][:], z_q[1][:]), True, True)
-            result = tile("result%d" % a, [P, V], F32)
-            copy(a == 1, result[:], acc[:])
-            (nc.sync if a == 1 else nc.scalar).dma_start(out=out[rows, :], in_=result[:])
+        half = V // 2
+        z_grouped = [tile("z_grouped%d" % u, [P, half, PACK], BF16) for u in range(2)]
+        for u in range(2):
+            nc.vector.tensor_tensor(
+                out=z_grouped[u][:].rearrange("p (c i) t -> p c t i", i=4),
+                in0=terms[:, :, u * half:(u + 1) * half].rearrange("p t (c i) -> p c t i", i=4),
+                in1=terms[:, :, V + u * half:V + (u + 1) * half].rearrange("p t (c i) -> p c t i", i=4),
+                op=ADD,
+            )
+        out_rows = out.rearrange("(a p) v -> p a v", p=P)
+        for u in range(2):
+            z_codes, z_scales = quantize("z%d" % u, z_grouped[u][:])
+            result = tile("result%d" % u, [P, N // P, half], F32)
+            for a in range(N // P):
+                rows = slice(a * P, (a + 1) * P)
+                acc = bank("out_acc%d%d" % (u, a), 1 + 2 * u + a, half)
+                matmul(acc[:], (w2_codes[:, rows], w2_scales[:, rows]), (z_codes[:], z_scales[:]), True, True)
+                copy(u == 1 and a == 1, result[:, a, :], acc[:])
+            nc.sync.dma_start(out=out_rows[:, :, u * half:(u + 1) * half], in_=result[:])

from contextlib import ExitStack

import concourse.mybir as mybir

K, T, S, V, H, N, J = 1024, 2048, 512, 256, 512, 256, 512
FLOPS = 2 * (K * H * S + J * H * 2 * V + H * N * V)

F32 = mybir.dt.float32
BF16 = mybir.dt.bfloat16
U32 = mybir.dt.uint32
U16 = mybir.dt.uint16
U8 = mybir.dt.uint8
FP8X4 = mybir.dt.float8_e4m3fn_x4
SILU = mybir.ActivationFunctionType.Silu
MULT = mybir.AluOpType.mult
ADD = mybir.AluOpType.add

P = 128
PACK = 4
K_PASS = P * PACK


def tile_picked_dime_none_e_kernel(tc, xT, aT, w1, w3, w2, offs, pos1, pos2, out):
    nc = tc.nc
    passes = K // K_PASS

    with ExitStack() as ctx:
        keep = ctx.enter_context(tc.tile_pool(name="keep", bufs=1))
        psum = ctx.enter_context(tc.psum_pool(name="psum", bufs=1))

        def tile(name, shape, dtype, tag=None):
            return keep.tile(shape, dtype, name=name, tag=tag or name, align_bytes=64)

        def quantize(name, grouped, tag=None):
            width = grouped.shape[1]
            codes = tile(name + "_codes", [P, width], U32, tag=tag)
            scales = tile(name + "_scales", [P, width], U8)
            nc.vector.quantize_mx(
                out=codes[:].bitcast(FP8X4), scales=scales[:], in_=grouped.rearrange("p w j -> p (w j)")
            )
            return codes, scales

        def matmul(acc, lhs, rhs, start, stop):
            nc.tensor.matmul_mx(
                out=acc, lhsT=lhs[0].bitcast(FP8X4), lhsT_scale=lhs[1],
                rhs=rhs[0].bitcast(FP8X4), rhs_scale=rhs[1], start=start, stop=stop,
            )

        def copy(on_vector, dst, src):
            if on_vector:
                nc.vector.tensor_copy(out=dst, in_=src)
            else:
                nc.scalar.copy(out=dst, in_=src)

        def group_columns(name, raw, on_vector):
            width = raw.shape[2]
            grouped = tile(name, [P, width, PACK], BF16)
            copy(on_vector,
                 grouped[:].rearrange("p (c i) j -> p c j i", i=4),
                 raw.rearrange("p j (c i) -> p c j i", i=4))
            return grouped[:]

        def group_channels(grouped, raw, t, on_vector):
            copy(on_vector,
                 grouped.rearrange("p (g h i) j -> p g h j i", h=2, i=4),
                 raw[:].rearrange("p j (g t h i) -> p t g h j i", t=PACK, h=2, i=4)[:, t])
            return grouped

        def load_rows(name, rows):
            raw = tile(name, [P, PACK, rows.shape[1]], F32)
            nc.sync.dma_start(out=raw[:], in_=rows.rearrange("(p j) w -> p j w", j=PACK))
            return raw

        def load_list(name, src):
            lst = keep.tile(list(src.shape), U16, name=name)
            nc.sync.dma_start(lst[:], src)
            return lst

        warm = tile("warm", [P, 8], F32)
        nc.vector.memset(warm[:], 0.0)
        warm2 = tile("warm2", [P, 8], F32)
        nc.scalar.activation(out=warm2[:], in_=warm[:], func=SILU)
        x_rows = xT.rearrange("(z p j) w -> z j p w", p=P, j=PACK)
        planes = {}
        for z in range(passes):
            for j in range(PACK):
                planes[z, j] = tile("x%d%d" % (z, j), [P, T], F32)
                nc.sync.dma_start(out=planes[z, j][:], in_=x_rows[z, j])
                if (z, j) == (0, 0):
                    picks = load_list("picks", offs)
                if (z, j) == (0, 1):
                    places = [load_list("places1", pos1), load_list("places2", pos2)]
        w1_raw = [load_rows("w1_raw%d" % z, w1[z * K_PASS:(z + 1) * K_PASS, :]) for z in range(passes)]
        a_raw = [load_rows("a_raw0", aT[:, 0:V])]
        w3_raw = load_rows("w3_raw", w3)
        a_raw.append(load_rows("a_raw1", aT[:, V:2 * V]))
        w2_raw = tile("w2_raw", [P, PACK, N], F32)
        w2_rows = w2.rearrange("(g t e) n -> t g e n", t=PACK, e=8)
        for t in range(PACK):
            nc.sync.dma_start(out=w2_raw[:, t, :], in_=w2_rows[t])

        x_grouped = [tile("x_grouped%d" % z, [P, S, PACK], BF16) for z in range(passes)]
        x_q = []
        for z in range(passes):
            for j in range(PACK):
                nc.vector.tensor_copy(out=x_grouped[z][:, :, j], in_=planes[z, j][:].indirect(picks[:]))

        def bank(name, b, width):
            return psum.tile([P, width], F32, name=name, tag="bank%d" % b)

        h_parts = [[(slice(0, S // 2), 0), (slice(S // 2, S), PACK)]] + [[(slice(0, S), t)] for t in range(1, PACK)]
        h_acc = [[bank("h_acc%d" % b, b, cols.stop - cols.start) for cols, b in parts] for parts in h_parts]
        h = [tile("h%d" % t, [P, S], F32) for t in range(PACK)]
        for z in range(passes):
            x_q.append(quantize("x%d" % z, x_grouped[z][:], tag="w1_g02" if z == 1 else None))
            for t in range(PACK):
                grouped = group_channels(tile("w1_g%d%d" % (z, t), [P, P, PACK], BF16)[:], w1_raw[z], t, t % 2 == 0)
                codes, scales = quantize("w1_%d%d" % (z, t), grouped)
                for (cols, b), acc in zip(h_parts[t], h_acc[t]):
                    matmul(acc[:], (codes[:], scales[:]), (x_q[z][0][:, cols], x_q[z][1][:, cols]), z == 0, z == passes - 1)

        fetched = []
        terms_flat = tile("terms", [P, PACK * 2 * V], F32)
        terms = terms_flat[:].rearrange("p (t v) -> p t v", t=PACK)
        a_grouped = [tile("a_grouped%d" % d, [P, V, PACK], BF16) for d in range(2)]
        a_codes = tile("a_codes", [P, 2 * V], U32)
        a_scales = tile("a_scales", [P, 2 * V], U8)

        def fetch(t):
            for (cols, b), acc in zip(h_parts[t], h_acc[t]):
                nc.scalar.activation(out=h[t][:, cols], in_=acc[:], func=SILU)
            fetched.append(tile("fetched%d" % t, [P, 2 * V], F32, tag="a_grouped1" if t == PACK - 1 else None))
            for d in range(2):
                nc.vector.tensor_copy(out=fetched[t][:, d * V:(d + 1) * V], in_=h[t][:].indirect(places[d][:]))

        def angles(d):
            cols = slice(d * V, (d + 1) * V)
            copy(d == 0, a_grouped[d][:].rearrange("p (c i) j -> p c j i", i=4),
                 a_raw[d][:].rearrange("p j (c i) -> p c j i", i=4))
            nc.vector.quantize_mx(out=a_codes[:, cols].bitcast(FP8X4), scales=a_scales[:, cols],
                                  in_=a_grouped[d][:].rearrange("p w j -> p (w j)"))

        def filters(pair, staged):
            for e in range(2):
                group_channels(staged[:, e * P:(e + 1) * P, :], w3_raw, 2 * pair + e, False)
            return quantize("w3_%d" % pair, staged)

        def filter_products(pair, w3_q):
            accs = []
            for e in range(2):
                acc = bank("f_acc%d%d" % (pair, e), PACK + 2 * pair + e, 2 * V)
                cols = slice(e * P, (e + 1) * P)
                matmul(acc[:], (w3_q[0][:, cols], w3_q[1][:, cols]), (a_codes[:], a_scales[:]), True, True)
                accs.append(acc)
            return accs

        angles(0)
        fetch(0)
        fetch(1)
        w3_first = filters(0, tile("w3_g0", [P, 2 * P, PACK], BF16)[:])
        fetch(2)
        angles(1)
        f_acc = filter_products(0, w3_first)
        fetch(3)
        staged = terms_flat[:, 0:2 * V].bitcast(BF16).rearrange("p (m j) -> p m j", j=PACK)
        f_acc.extend(filter_products(1, filters(1, staged)))
        for t in range(PACK):
            nc.vector.tensor_tensor(out=terms_flat[:, t * 2 * V:(t + 1) * 2 * V], in0=fetched[t][:], in1=f_acc[t][:], op=MULT)
        w2_codes, w2_scales = quantize("w2", group_columns("w2_g", w2_raw[:], False))

        half = V // 2
        z_grouped = [tile("z_grouped%d" % u, [P, half, PACK], BF16) for u in range(2)]
        for u in range(2):
            nc.vector.tensor_tensor(
                out=z_grouped[u][:].rearrange("p (c i) t -> p c t i", i=4),
                in0=terms[:, :, u * half:(u + 1) * half].rearrange("p t (c i) -> p c t i", i=4),
                in1=terms[:, :, V + u * half:V + (u + 1) * half].rearrange("p t (c i) -> p c t i", i=4),
                op=ADD,
            )
        out_rows = out.rearrange("(a p) v -> p a v", p=P)
        for u in range(2):
            z_codes, z_scales = quantize("z%d" % u, z_grouped[u][:])
            result = tile("result%d" % u, [P, N // P, half], F32)
            for a in range(N // P):
                rows = slice(a * P, (a + 1) * P)
                acc = bank("out_acc%d%d" % (u, a), 1 + 2 * u + a, half)
                matmul(acc[:], (w2_codes[:, rows], w2_scales[:, rows]), (z_codes[:], z_scales[:]), True, True)
                copy(u == 1 and a == 1, result[:, a, :], acc[:])
            nc.sync.dma_start(out=out_rows[:, :, u * half:(u + 1) * half], in_=result[:])
